import numpy as np
import ml_dtypes


def mxq(x, axis, fmt="e4m3"):
    dtype, down = {"e4m3": (ml_dtypes.float8_e4m3fn, 7), "e5m2": (ml_dtypes.float8_e5m2, 14)}[fmt]
    v = np.moveaxis(np.asarray(x, np.float32).astype(ml_dtypes.bfloat16).astype(np.float64), axis, -1)
    blocks = v.reshape(v.shape[:-1] + (-1, 32))
    amax = np.abs(blocks).max(-1, keepdims=True)
    byte = np.maximum(np.where(amax > 0, np.frexp(amax)[1] - 1 + 127, 0) - down, 1)
    scale = np.exp2(byte - 127.0)
    codes = (blocks / scale).astype(np.float32).astype(dtype).astype(np.float64)
    return np.moveaxis((codes * scale).reshape(v.shape), -1, axis)


WIDE = False


def mx_kscale(k):
    if not WIDE:
        return np.ones(k)
    levels = np.array([10, -10, 5, -5, 0])
    if k % 512:
        return np.exp2(np.random.permutation(np.resize(levels, k // 32))).repeat(32)
    a = np.empty((k // 512, 16))
    for p in range(k // 512):
        a[p, :8] = np.random.permutation(np.resize(levels, 8))
        for g in range(8):
            far = levels[np.abs(levels - a[p, g]) >= 10]
            a[p, g + 8] = far[np.random.randint(len(far))]
    return np.exp2(a.ravel()).repeat(32)


def f64(x):
    return np.asarray(x).astype(np.float64)


def striped(idx):
    return np.tile(idx.reshape(-1, 16).T, (8, 1)).astype(np.uint16)


def unstriped(offs):
    return offs[:16].T.reshape(-1).astype(np.int64)


def pack_weight(w):
    k, n = w.shape
    w = f64(np.asarray(w, np.float32).astype(ml_dtypes.bfloat16)).reshape(k // 32, 32, n)
    amax = np.abs(w).max(1)
    byte = np.clip(np.where(amax > 0, np.frexp(amax)[1] - 1 + 127 - 7, 1), 1, 254)
    scaled = (w * np.exp2(127.0 - byte)[:, None, :]).reshape(k, n).astype(np.float32)
    words = np.ascontiguousarray(scaled.reshape(k // 512, 128, 4, n).transpose(0, 1, 3, 2)).astype(ml_dtypes.float8_e4m3fn).view(np.uint8)
    return words, np.ascontiguousarray(byte.astype(np.uint8).reshape(k // 512, 16, n))


def unpack_weight(words, scales):
    g, p, n, _ = words.shape
    vals = np.ascontiguousarray(words).view(ml_dtypes.float8_e4m3fn).astype(np.float64) * np.repeat(np.exp2(scales.astype(np.float64) - 127.0), 8, axis=1)[..., None]
    return vals.transpose(0, 1, 3, 2).reshape(g * 512, n)


def planes(y):
    n, m = y.shape
    v = y.astype(np.float32).astype(ml_dtypes.bfloat16).astype(np.float64).reshape(n // 32, 32, m)
    top = np.abs(v).max(1)
    byte = np.clip(np.where(top > 0, np.frexp(top)[1] - 1 + 127 - 7, 1), 1, 254)
    codes = (v * np.exp2(127.0 - byte)[:, None, :]).reshape(n, m).astype(np.float32).astype(ml_dtypes.float8_e4m3fn).view(np.uint8)
    words = codes.reshape(n // 512, 128, 4, m).transpose(0, 1, 3, 2)
    return np.ascontiguousarray(words), np.ascontiguousarray(byte.astype(np.uint8).reshape(n // 512, 16, m))


def gelu(v):
    return 0.5 * v * (1.0 + np.tanh(np.sqrt(2.0 / np.pi) * (v + 0.044715 * v**3)))


K, T, S, H = 512, 1024, 512, 512


def setup_inputs():
    n = np.random.standard_normal
    s = mx_kscale(K)[:, None]
    u = mx_kscale(H)
    packed_xT = pack_weight(n((K, T)) * s)
    return {
        "x_words": packed_xT[0],
        "x_scales": packed_xT[1],
        "w1": (n((K, H)) / np.sqrt(K) / s * u).astype(np.float32),
        "w2": (n((H, H)) / np.sqrt(H) / u[:, None]).astype(np.float32),
        "turn": (np.random.uniform(0.5, 1.5, (H, 1)) * u[:, None]).astype(np.float32),
        "offs": striped(np.random.permutation(T)[:S]),
    }


def reference(x_words, x_scales, w1, w2, turn, offs):
    xq = unpack_weight(x_words, x_scales)[:, unstriped(offs)]
    h = mxq(f64(w1), 0, "e4m3").T @ xq
    g = gelu(h)
    y = mxq(f64(w2), 0, "e4m3").T @ mxq(g, 0, "e4m3")
    out_0 = h + f64(turn) * y
    return (out_0,) + planes(out_0)

@@ -1,0 +1,134 @@
+from contextlib import ExitStack
+
+import concourse.mybir as mybir
+
+F32 = mybir.dt.float32
+BF16 = mybir.dt.bfloat16
+I32 = mybir.dt.int32
+U32 = mybir.dt.uint32
+U16 = mybir.dt.uint16
+U8 = mybir.dt.uint8
+FP8X4 = mybir.dt.float8_e4m3fn_x4
+GELU = mybir.ActivationFunctionType.Gelu_apprx_tanh
+MULT = mybir.AluOpType.mult
+ADD = mybir.AluOpType.add
+
+P = 128
+PACK = 4
+WIDTH = 512
+STORED = 1024
+PICKED = 512
+CHUNK = 128
+CHUNKS = PICKED // CHUNK
+HALF = WIDTH // 2
+QUADRANTS = 4
+
+FLOPS = 2 * 2 * WIDTH * WIDTH * PICKED
+
+
+def tile_picked_zres_gelu_po_kernel(tc, x_words, x_scales, w1, w2, turn, offs, out_0, out_1, out_2):
+    nc = tc.nc
+    with ExitStack() as ctx:
+        keep = ctx.enter_context(tc.tile_pool(name="keep", bufs=1))
+        psum = ctx.enter_context(tc.psum_pool(name="psum", bufs=1))
+
+        def load_weight_half(w, half, name):
+            raw = keep.tile([P, PACK, HALF], F32, name=name)
+            nc.sync.dma_start(out=raw[:], in_=w.rearrange("(p j) c -> p j c", j=PACK)[:, :, half * HALF : (half + 1) * HALF])
+            return raw
+
+        def deal_weight_half(copy, grouped, raw, half):
+            rows = slice(half * HALF // PACK, (half + 1) * HALF // PACK)
+            copy(out=grouped[:, :, rows, :].rearrange("p t m j -> p m t j"), in_=raw[:].rearrange("p j (m t) -> p m t j", t=PACK))
+
+        def quantise(grouped_flat, codes, scales):
+            nc.vector.quantize_mx(out=codes.bitcast(FP8X4), scales=scales, in_=grouped_flat)
+
+        def product(bank, w_codes, w_scales, codes, scales):
+            for t in range(PACK):
+                cols = slice(t * P, (t + 1) * P)
+                nc.tensor.matmul_mx(out=bank[:, t, :], lhsT=w_codes[:, cols].bitcast(FP8X4), lhsT_scale=w_scales[:, cols],
+                                    rhs=codes.bitcast(FP8X4), rhs_scale=scales, start=True, stop=True)
+
+        stored_scales = keep.tile([P, STORED], U8, align_bytes=64)
+        nc.vector.memset(stored_scales[:].bitcast(I32), 0)
+        warm_in = keep.tile([P, 1], F32)
+        nc.gpsimd.memset(warm_in[:], 0.0)
+        warm_out = keep.tile([P, 1], F32)
+        nc.scalar.activation(out=warm_out[:], in_=warm_in[:], func=GELU)
+
+        offsets = keep.tile([P, PICKED // 16], U16)
+        nc.sync.dma_start(offsets[:], offs)
+        w1_raw = [load_weight_half(w1, 0, "w1_raw0")]
+        for q in range(QUADRANTS):
+            nc.sync.dma_start(out=stored_scales[32 * q : 32 * q + 4, :].bitcast(I32), in_=x_scales[0, 4 * q : 4 * q + 4, :].bitcast(I32))
+        w1_raw.append(load_weight_half(w1, 1, "w1_raw1"))
+        stored_words = keep.tile([P, STORED], I32, align_bytes=64)
+        nc.sync.dma_start(out=stored_words[:], in_=x_words[0].rearrange("p n t -> p (n t)").bitcast(I32))
+        w2_raw = [load_weight_half(w2, half, "w2_raw%d" % half) for half in range(2)]
+        turn_cols = keep.tile([P, PACK], F32)
+        nc.sync.dma_start(out=turn_cols[:], in_=turn.rearrange("(p t) o -> p (t o)", t=PACK))
+
+        x_scale = keep.tile([P, PICKED], U8, align_bytes=64)
+        nc.vector.tensor_copy(out=x_scale[:], in_=stored_scales[:].indirect(offsets[:]))
+
+        w1_grouped = keep.tile([P, PACK, P, PACK], BF16, align_bytes=64)
+        deal_weight_half(nc.scalar.copy, w1_grouped, w1_raw[0], 0)
+        deal_weight_half(nc.vector.tensor_copy, w1_grouped, w1_raw[1], 1)
+        w1_codes = keep.tile([P, WIDTH], U32, align_bytes=64)
+        w1_scale = keep.tile([P, WIDTH], U8, align_bytes=64)
+        quantise(w1_grouped[:].rearrange("p t m j -> p (t m j)"), w1_codes[:], w1_scale[:])
+
+        h_banks, g_grouped = [], []
+        for c in range(CHUNKS):
+            cols = slice(c * CHUNK, (c + 1) * CHUNK)
+            x_codes = keep.tile([P, CHUNK], U32, name="x_codes%d" % c, align_bytes=64)
+            nc.vector.tensor_copy(out=x_codes[:], in_=stored_words[:].bitcast(U32).indirect(offsets[:, c * CHUNK // 16 : (c + 1) * CHUNK // 16]))
+            bank = psum.tile([P, PACK, CHUNK], F32, name="h_bank%d" % c)
+            product(bank, w1_codes, w1_scale, x_codes[:], x_scale[:, cols])
+            grouped = keep.tile([P, CHUNK, PACK], BF16, name="g_grouped%d" % c, align_bytes=64)
+            nc.scalar.activation(out=grouped[:], in_=bank[:].rearrange("p t n -> p n t"), func=GELU)
+            h_banks.append(bank)
+            g_grouped.append(grouped)
+
+        w2_grouped = keep.tile([P, PACK, P, PACK], BF16, align_bytes=64)
+        for half in range(2):
+            deal_weight_half(nc.vector.tensor_copy, w2_grouped, w2_raw[half], half)
+        w2_codes = keep.tile([P, WIDTH], U32, align_bytes=64)
+        w2_scale = keep.tile([P, WIDTH], U8, align_bytes=64)
+        quantise(w2_grouped[:].rearrange("p t m j -> p (t m j)"), w2_codes[:], w2_scale[:])
+
+        h_rows, y_banks = [], []
+        for c in range(CHUNKS):
+            h = keep.tile([P, PACK, CHUNK], F32, name="h%d" % c)
+            nc.scalar.copy(out=h[:], in_=h_banks[c][:])
+            h_rows.append(h)
+            g_codes = keep.tile([P, CHUNK], U32, name="g_codes%d" % c, align_bytes=64)
+            g_scale = keep.tile([P, CHUNK], U8, name="g_scale%d" % c, align_bytes=64)
+            quantise(g_grouped[c][:].rearrange("p n t -> p (n t)"), g_codes[:], g_scale[:])
+            bank = psum.tile([P, PACK, CHUNK], F32, name="y_bank%d" % c)
+            product(bank, w2_codes, w2_scale, g_codes[:], g_scale[:])
+            y_banks.append(bank)
+
+        out_rows = out_0.rearrange("(p t) n -> p t n", t=PACK)
+        out_words = out_1[0].rearrange("p n t -> p (n t)").bitcast(I32)
+        out_scale = keep.tile([P, PICKED], U8, align_bytes=64)
+        results = []
+        for c in range(CHUNKS):
+            result = keep.tile([P, PACK, CHUNK], F32, name="result%d" % c)
+            for t in range(PACK):
+                nc.vector.scalar_tensor_tensor(out=result[:, t, :], in0=y_banks[c][:, t, :], scalar=turn_cols[:, t : t + 1],
+                                               in1=h_rows[c][:, t, :], op0=MULT, op1=ADD)
+            nc.sync.dma_start(out=out_rows[:, :, c * CHUNK : (c + 1) * CHUNK], in_=result[:])
+            results.append(result)
+        for c in range(CHUNKS):
+            cols = slice(c * CHUNK, (c + 1) * CHUNK)
+            grouped = keep.tile([P, CHUNK, PACK], BF16, name="out_grouped%d" % c, align_bytes=64)
+            copy = nc.vector.tensor_copy if c == CHUNKS - 1 else nc.scalar.copy
+            copy(out=grouped[:].rearrange("p (a i) t -> p a t i", i=4), in_=results[c][:].rearrange("p t (a i) -> p a t i", i=4))
+            out_codes = keep.tile([P, CHUNK], U32, name="out_codes%d" % c, align_bytes=64)
+            quantise(grouped[:].rearrange("p n t -> p (n t)"), out_codes[:], out_scale[:, cols])
+            nc.sync.dma_start(out=out_words[:, cols], in_=out_codes[:].bitcast(I32))
+        for q in range(QUADRANTS):
+            queue = nc.sync if q % 2 == 0 else nc.scalar
+            queue.dma_start(out=out_2[0, 4 * q : 4 * q + 4, :].bitcast(I32), in_=out_scale[32 * q : 32 * q + 4, :].bitcast(I32))

@@ -33,16 +33,21 @@ def tile_picked_zres_gelu_po_kernel(tc, x_words, x_scales, w1, w2, turn, offs, o
         psum = ctx.enter_context(tc.psum_pool(name="psum", bufs=1))
 
         def load_weight_half(w, half, name):
-            raw = keep.tile([P, PACK, HALF], F32, name=name)
+            raw = keep.tile([P, PACK, HALF], F32, name=name, tag=name, align_bytes=64)
             nc.sync.dma_start(out=raw[:], in_=w.rearrange("(p j) c -> p j c", j=PACK)[:, :, half * HALF : (half + 1) * HALF])
             return raw
 
-        def deal_weight_half(copy, grouped, raw, half):
-            rows = slice(half * HALF // PACK, (half + 1) * HALF // PACK)
-            copy(out=grouped[:, :, rows, :].rearrange("p t m j -> p m t j"), in_=raw[:].rearrange("p j (m t) -> p m t j", t=PACK))
+        def deal_weight(copy, grouped, raw, half, first, last):
+            base = half * HALF // PACK
+            copy(out=grouped[:, :, base + first : base + last, :].rearrange("p t m j -> p m t j"),
+                 in_=raw[:].rearrange("p j (m t) -> p m t j", t=PACK)[:, first:last])
 
         def quantise(grouped_flat, codes, scales):
             nc.vector.quantize_mx(out=codes.bitcast(FP8X4), scales=scales, in_=grouped_flat)
+
+        def quantise_slot(grouped, codes, scales, t):
+            slot = slice(t * P, (t + 1) * P)
+            quantise(grouped[:, t].rearrange("p m j -> p (m j)"), codes[:, slot], scales[:, slot])
 
         def product(bank, w_codes, w_scales, codes, scales):
             for t in range(PACK):
@@ -73,11 +78,14 @@ def tile_picked_zres_gelu_po_kernel(tc, x_words, x_scales, w1, w2, turn, offs, o
         nc.vector.tensor_copy(out=x_scale[:], in_=stored_scales[:].indirect(offsets[:]))
 
         w1_grouped = keep.tile([P, PACK, P, PACK], BF16, align_bytes=64)
-        deal_weight_half(nc.scalar.copy, w1_grouped, w1_raw[0], 0)
-        deal_weight_half(nc.vector.tensor_copy, w1_grouped, w1_raw[1], 1)
+        deal_weight(nc.scalar.copy, w1_grouped, w1_raw[0], 0, 0, 64)
+        deal_weight(nc.vector.tensor_copy, w1_grouped, w1_raw[1], 1, 0, 32)
+        deal_weight(nc.scalar.copy, w1_grouped, w1_raw[1], 1, 32, 64)
         w1_codes = keep.tile([P, WIDTH], U32, align_bytes=64)
         w1_scale = keep.tile([P, WIDTH], U8, align_bytes=64)
         quantise(w1_grouped[:].rearrange("p t m j -> p (t m j)"), w1_codes[:], w1_scale[:])
+
+        w2_grouped = keep.tile([P, PACK, P, PACK], BF16, tag="w2_grouped", align_bytes=64)
 
         h_banks, g_grouped = [], []
         for c in range(CHUNKS):
@@ -91,24 +99,27 @@ def tile_picked_zres_gelu_po_kernel(tc, x_words, x_scales, w1, w2, turn, offs, o
             h_banks.append(bank)
             g_grouped.append(grouped)
 
-        w2_grouped = keep.tile([P, PACK, P, PACK], BF16, align_bytes=64)
-        for half in range(2):
-            deal_weight_half(nc.vector.tensor_copy, w2_grouped, w2_raw[half], half)
+        deal_weight(nc.vector.tensor_copy, w2_grouped, w2_raw[0], 0, 0, 64)
+        deal_weight(nc.vector.tensor_copy, w2_grouped, w2_raw[1], 1, 0, 64)
         w2_codes = keep.tile([P, WIDTH], U32, align_bytes=64)
         w2_scale = keep.tile([P, WIDTH], U8, align_bytes=64)
-        quantise(w2_grouped[:].rearrange("p t m j -> p (t m j)"), w2_codes[:], w2_scale[:])
+        g_codes = keep.tile([P, PICKED], U32, tag="w2_raw1", align_bytes=64)
+        g_scale = keep.tile([P, PICKED], U8, align_bytes=64)
 
         h_rows, y_banks = [], []
+        for c in range(CHUNKS):
+            cols = slice(c * CHUNK, (c + 1) * CHUNK)
+            quantise(g_grouped[c][:].rearrange("p n t -> p (n t)"), g_codes[:, cols], g_scale[:, cols])
+            if c == 0:
+                for t in range(PACK):
+                    quantise_slot(w2_grouped, w2_codes, w2_scale, t)
+            bank = psum.tile([P, PACK, CHUNK], F32, name="y_bank%d" % c)
+            product(bank, w2_codes, w2_scale, g_codes[:, cols], g_scale[:, cols])
+            y_banks.append(bank)
         for c in range(CHUNKS):
             h = keep.tile([P, PACK, CHUNK], F32, name="h%d" % c)
             nc.scalar.copy(out=h[:], in_=h_banks[c][:])
             h_rows.append(h)
-            g_codes = keep.tile([P, CHUNK], U32, name="g_codes%d" % c, align_bytes=64)
-            g_scale = keep.tile([P, CHUNK], U8, name="g_scale%d" % c, align_bytes=64)
-            quantise(g_grouped[c][:].rearrange("p n t -> p (n t)"), g_codes[:], g_scale[:])
-            bank = psum.tile([P, PACK, CHUNK], F32, name="y_bank%d" % c)
-            product(bank, w2_codes, w2_scale, g_codes[:], g_scale[:])
-            y_banks.append(bank)
 
         out_rows = out_0.rearrange("(p t) n -> p t n", t=PACK)
         out_words = out_1[0].rearrange("p n t -> p (n t)").bitcast(I32)
@@ -121,14 +132,21 @@ def tile_picked_zres_gelu_po_kernel(tc, x_words, x_scales, w1, w2, turn, offs, o
                                                in1=h_rows[c][:, t, :], op0=MULT, op1=ADD)
             nc.sync.dma_start(out=out_rows[:, :, c * CHUNK : (c + 1) * CHUNK], in_=result[:])
             results.append(result)
+        out_grouped = keep.tile([P, PICKED * PACK], BF16, align_bytes=64)
+        out_codes = keep.tile([P, PICKED], U32, align_bytes=64)
         for c in range(CHUNKS):
-            cols = slice(c * CHUNK, (c + 1) * CHUNK)
-            grouped = keep.tile([P, CHUNK, PACK], BF16, name="out_grouped%d" % c, align_bytes=64)
-            copy = nc.vector.tensor_copy if c == CHUNKS - 1 else nc.scalar.copy
-            copy(out=grouped[:].rearrange("p (a i) t -> p a t i", i=4), in_=results[c][:].rearrange("p t (a i) -> p a t i", i=4))
-            out_codes = keep.tile([P, CHUNK], U32, name="out_codes%d" % c, align_bytes=64)
-            quantise(grouped[:].rearrange("p n t -> p (n t)"), out_codes[:], out_scale[:, cols])
-            nc.sync.dma_start(out=out_words[:, cols], in_=out_codes[:].bitcast(I32))
+            grouped = out_grouped[:, c * CHUNK * PACK : (c + 1) * CHUNK * PACK]
+            if c < CHUNKS // 2:
+                nc.gpsimd.tensor_scalar(out=grouped.rearrange("p (n t) -> p n t", t=PACK), in0=results[c][:].rearrange("p t n -> p n t"),
+                                        scalar1=1.0, scalar2=-0.0, op0=MULT, op1=ADD)
+            else:
+                nc.scalar.copy(out=grouped.rearrange("p (a i t) -> p a t i", i=4, t=PACK), in_=results[c][:].rearrange("p t (a i) -> p a t i", i=4))
+        for first, last in ((0, 2), (2, 3), (3, 4)):
+            cols = slice(first * CHUNK, last * CHUNK)
+            quantise(out_grouped[:, first * CHUNK * PACK : last * CHUNK * PACK], out_codes[:, cols], out_scale[:, cols])
+        for half in range(2):
+            cols = slice(half * PICKED // 2, (half + 1) * PICKED // 2)
+            nc.sync.dma_start(out=out_words[:, cols], in_=out_codes[:, cols].bitcast(I32))
         for q in range(QUADRANTS):
             queue = nc.sync if q % 2 == 0 else nc.scalar
             queue.dma_start(out=out_2[0, 4 * q : 4 * q + 4, :].bitcast(I32), in_=out_scale[32 * q : 32 * q + 4, :].bitcast(I32))

@@ -39,8 +39,8 @@ def tile_picked_zres_gelu_po_kernel(tc, x_words, x_scales, w1, w2, turn, offs, o
 
         def deal_weight(copy, grouped, raw, half, first, last):
             base = half * HALF // PACK
-            copy(out=grouped[:, :, base + first : base + last, :].rearrange("p t m j -> p m t j"),
-                 in_=raw[:].rearrange("p j (m t) -> p m t j", t=PACK)[:, first:last])
+            copy(out=grouped[:, :, base + first : base + last, :].rearrange("p (u e) m j -> p u m j e", e=2),
+                 in_=raw[:].rearrange("p j (m u e) -> p u m j e", u=2, e=2)[:, :, first:last])
 
         def quantise(grouped_flat, codes, scales):
             nc.vector.quantize_mx(out=codes.bitcast(FP8X4), scales=scales, in_=grouped_flat)

@@ -45,9 +45,10 @@ def tile_picked_zres_gelu_po_kernel(tc, x_words, x_scales, w1, w2, turn, offs, o
         def quantise(grouped_flat, codes, scales):
             nc.vector.quantize_mx(out=codes.bitcast(FP8X4), scales=scales, in_=grouped_flat)
 
-        def quantise_slot(grouped, codes, scales, t):
-            slot = slice(t * P, (t + 1) * P)
-            quantise(grouped[:, t].rearrange("p m j -> p (m j)"), codes[:, slot], scales[:, slot])
+        def quantise_half(grouped, codes, scales, half):
+            for t in range(PACK):
+                cols = slice(t * P + half * 64, t * P + (half + 1) * 64)
+                quantise(grouped[:, t, half * 64 : (half + 1) * 64].rearrange("p m j -> p (m j)"), codes[:, cols], scales[:, cols])
 
         def product(bank, w_codes, w_scales, codes, scales):
             for t in range(PACK):
@@ -87,56 +88,69 @@ def tile_picked_zres_gelu_po_kernel(tc, x_words, x_scales, w1, w2, turn, offs, o
 
         w2_grouped = keep.tile([P, PACK, P, PACK], BF16, tag="w2_grouped", align_bytes=64)
 
-        h_banks, g_grouped = [], []
+        h_banks, g_grouped, h_rows, y_banks, results = [], [], [], [], []
+
+        def copy_h(c):
+            h = keep.tile([P, PACK, CHUNK], F32, name="h%d" % c)
+            nc.scalar.copy(out=h[:], in_=h_banks[c][:])
+            h_rows.append(h)
+
         for c in range(CHUNKS):
             cols = slice(c * CHUNK, (c + 1) * CHUNK)
             x_codes = keep.tile([P, CHUNK], U32, name="x_codes%d" % c, align_bytes=64)
             nc.vector.tensor_copy(out=x_codes[:], in_=stored_words[:].bitcast(U32).indirect(offsets[:, c * CHUNK // 16 : (c + 1) * CHUNK // 16]))
             bank = psum.tile([P, PACK, CHUNK], F32, name="h_bank%d" % c)
             product(bank, w1_codes, w1_scale, x_codes[:], x_scale[:, cols])
+            h_banks.append(bank)
+            if c == CHUNKS - 1:
+                copy_h(0)
             grouped = keep.tile([P, CHUNK, PACK], BF16, name="g_grouped%d" % c, align_bytes=64)
             nc.scalar.activation(out=grouped[:], in_=bank[:].rearrange("p t n -> p n t"), func=GELU)
-            h_banks.append(bank)
             g_grouped.append(grouped)
+        for c in range(1, CHUNKS):
+            copy_h(c)
 
-        deal_weight(nc.vector.tensor_copy, w2_grouped, w2_raw[0], 0, 0, 64)
-        deal_weight(nc.vector.tensor_copy, w2_grouped, w2_raw[1], 1, 0, 64)
         w2_codes = keep.tile([P, WIDTH], U32, align_bytes=64)
         w2_scale = keep.tile([P, WIDTH], U8, align_bytes=64)
+        deal_weight(nc.vector.tensor_copy, w2_grouped, w2_raw[0], 0, 0, 64)
+        quantise_half(w2_grouped, w2_codes, w2_scale, 0)
+        deal_weight(nc.vector.tensor_copy, w2_grouped, w2_raw[1], 1, 0, 64)
         g_codes = keep.tile([P, PICKED], U32, tag="w2_raw1", align_bytes=64)
         g_scale = keep.tile([P, PICKED], U8, align_bytes=64)
-
-        h_rows, y_banks = [], []
-        for c in range(CHUNKS):
-            cols = slice(c * CHUNK, (c + 1) * CHUNK)
-            quantise(g_grouped[c][:].rearrange("p n t -> p (n t)"), g_codes[:, cols], g_scale[:, cols])
-            if c == 0:
-                for t in range(PACK):
-                    quantise_slot(w2_grouped, w2_codes, w2_scale, t)
-            bank = psum.tile([P, PACK, CHUNK], F32, name="y_bank%d" % c)
-            product(bank, w2_codes, w2_scale, g_codes[:, cols], g_scale[:, cols])
-            y_banks.append(bank)
-        for c in range(CHUNKS):
-            h = keep.tile([P, PACK, CHUNK], F32, name="h%d" % c)
-            nc.scalar.copy(out=h[:], in_=h_banks[c][:])
-            h_rows.append(h)
 
         out_rows = out_0.rearrange("(p t) n -> p t n", t=PACK)
         out_words = out_1[0].rearrange("p n t -> p (n t)").bitcast(I32)
         out_scale = keep.tile([P, PICKED], U8, align_bytes=64)
-        results = []
-        for c in range(CHUNKS):
+
+        def second_product(c):
+            cols = slice(c * CHUNK, (c + 1) * CHUNK)
+            quantise(g_grouped[c][:].rearrange("p n t -> p (n t)"), g_codes[:, cols], g_scale[:, cols])
+            if c == 0:
+                quantise_half(w2_grouped, w2_codes, w2_scale, 1)
+            bank = psum.tile([P, PACK, CHUNK], F32, name="y_bank%d" % c)
+            product(bank, w2_codes, w2_scale, g_codes[:, cols], g_scale[:, cols])
+            y_banks.append(bank)
+
+        def combine(c):
             result = keep.tile([P, PACK, CHUNK], F32, name="result%d" % c)
             for t in range(PACK):
                 nc.vector.scalar_tensor_tensor(out=result[:, t, :], in0=y_banks[c][:, t, :], scalar=turn_cols[:, t : t + 1],
                                                in1=h_rows[c][:, t, :], op0=MULT, op1=ADD)
             nc.sync.dma_start(out=out_rows[:, :, c * CHUNK : (c + 1) * CHUNK], in_=result[:])
             results.append(result)
+
+        for c in range(CHUNKS - 1):
+            second_product(c)
+        combine(0)
+        second_product(CHUNKS - 1)
+        for c in range(1, CHUNKS):
+            combine(c)
+
         out_grouped = keep.tile([P, PICKED * PACK], BF16, align_bytes=64)
         out_codes = keep.tile([P, PICKED], U32, align_bytes=64)
         for c in range(CHUNKS):
             grouped = out_grouped[:, c * CHUNK * PACK : (c + 1) * CHUNK * PACK]
-            if c < CHUNKS // 2:
+            if c == 0:
                 nc.gpsimd.tensor_scalar(out=grouped.rearrange("p (n t) -> p n t", t=PACK), in0=results[c][:].rearrange("p t n -> p n t"),
                                         scalar1=1.0, scalar2=-0.0, op0=MULT, op1=ADD)
             else:

@@ -20,8 +20,16 @@ STORED = 1024
 PICKED = 512
 CHUNK = 128
 CHUNKS = PICKED // CHUNK
-HALF = WIDTH // 2
+LIST_ROWS = 16
 QUADRANTS = 4
+QUADRANT = P // QUADRANTS
+SCALE_ROWS = 4
+HALF = WIDTH // 2
+HALF_SLOT = HALF // PACK
+ALIGN = 64
+
+VECTOR_SHARE = 40
+W2_PIECES = ((0, 256), (256, 384), (384, 512))
 
 FLOPS = 2 * 2 * WIDTH * WIDTH * PICKED
 
@@ -32,23 +40,22 @@ def tile_picked_zres_gelu_po_kernel(tc, x_words, x_scales, w1, w2, turn, offs, o
         keep = ctx.enter_context(tc.tile_pool(name="keep", bufs=1))
         psum = ctx.enter_context(tc.psum_pool(name="psum", bufs=1))
 
-        def load_weight_half(w, half, name):
-            raw = keep.tile([P, PACK, HALF], F32, name=name, tag=name, align_bytes=64)
-            nc.sync.dma_start(out=raw[:], in_=w.rearrange("(p j) c -> p j c", j=PACK)[:, :, half * HALF : (half + 1) * HALF])
+        def load_weight_piece(w, first, last, name):
+            raw = keep.tile([P, PACK, last - first], F32, name=name, tag=name, align_bytes=ALIGN)
+            nc.sync.dma_start(out=raw[:], in_=w.rearrange("(p j) c -> p j c", j=PACK)[:, :, first:last])
             return raw
 
-        def deal_weight(copy, grouped, raw, half, first, last):
-            base = half * HALF // PACK
+        def deal_weight(copy, grouped, raw, base, first, last):
             copy(out=grouped[:, :, base + first : base + last, :].rearrange("p (u e) m j -> p u m j e", e=2),
                  in_=raw[:].rearrange("p j (m u e) -> p u m j e", u=2, e=2)[:, :, first:last])
 
-        def quantise(grouped_flat, codes, scales):
-            nc.vector.quantize_mx(out=codes.bitcast(FP8X4), scales=scales, in_=grouped_flat)
+        def quantise(values, codes, scales):
+            nc.vector.quantize_mx(out=codes.bitcast(FP8X4), scales=scales, in_=values)
 
         def quantise_half(grouped, codes, scales, half):
             for t in range(PACK):
-                cols = slice(t * P + half * 64, t * P + (half + 1) * 64)
-                quantise(grouped[:, t, half * 64 : (half + 1) * 64].rearrange("p m j -> p (m j)"), codes[:, cols], scales[:, cols])
+                cols = slice(t * P + half * HALF_SLOT, t * P + (half + 1) * HALF_SLOT)
+                quantise(grouped[:, t, half * HALF_SLOT : (half + 1) * HALF_SLOT].rearrange("p m j -> p (m j)"), codes[:, cols], scales[:, cols])
 
         def product(bank, w_codes, w_scales, codes, scales):
             for t in range(PACK):
@@ -56,37 +63,34 @@ def tile_picked_zres_gelu_po_kernel(tc, x_words, x_scales, w1, w2, turn, offs, o
                 nc.tensor.matmul_mx(out=bank[:, t, :], lhsT=w_codes[:, cols].bitcast(FP8X4), lhsT_scale=w_scales[:, cols],
                                     rhs=codes.bitcast(FP8X4), rhs_scale=scales, start=True, stop=True)
 
-        stored_scales = keep.tile([P, STORED], U8, align_bytes=64)
+        stored_scales = keep.tile([P, STORED], U8, align_bytes=ALIGN)
         nc.vector.memset(stored_scales[:].bitcast(I32), 0)
-        warm_in = keep.tile([P, 1], F32)
-        nc.gpsimd.memset(warm_in[:], 0.0)
-        warm_out = keep.tile([P, 1], F32)
-        nc.scalar.activation(out=warm_out[:], in_=warm_in[:], func=GELU)
 
-        offsets = keep.tile([P, PICKED // 16], U16)
+        offsets = keep.tile([P, PICKED // LIST_ROWS], U16)
         nc.sync.dma_start(offsets[:], offs)
-        w1_raw = [load_weight_half(w1, 0, "w1_raw0")]
+        w1_raw = [load_weight_piece(w1, 0, HALF, "w1_raw0")]
         for q in range(QUADRANTS):
-            nc.sync.dma_start(out=stored_scales[32 * q : 32 * q + 4, :].bitcast(I32), in_=x_scales[0, 4 * q : 4 * q + 4, :].bitcast(I32))
-        w1_raw.append(load_weight_half(w1, 1, "w1_raw1"))
-        stored_words = keep.tile([P, STORED], I32, align_bytes=64)
+            nc.sync.dma_start(out=stored_scales[QUADRANT * q : QUADRANT * q + SCALE_ROWS, :].bitcast(I32),
+                              in_=x_scales[0, SCALE_ROWS * q : SCALE_ROWS * (q + 1), :].bitcast(I32))
+        w1_raw.append(load_weight_piece(w1, HALF, WIDTH, "w1_raw1"))
+        stored_words = keep.tile([P, STORED], I32, align_bytes=ALIGN)
         nc.sync.dma_start(out=stored_words[:], in_=x_words[0].rearrange("p n t -> p (n t)").bitcast(I32))
-        w2_raw = [load_weight_half(w2, half, "w2_raw%d" % half) for half in range(2)]
+        w2_raw = [load_weight_piece(w2, first, last, "w2_raw%d" % i) for i, (first, last) in enumerate(W2_PIECES)]
         turn_cols = keep.tile([P, PACK], F32)
         nc.sync.dma_start(out=turn_cols[:], in_=turn.rearrange("(p t) o -> p (t o)", t=PACK))
 
-        x_scale = keep.tile([P, PICKED], U8, align_bytes=64)
+        x_scale = keep.tile([P, PICKED], U8, align_bytes=ALIGN)
         nc.vector.tensor_copy(out=x_scale[:], in_=stored_scales[:].indirect(offsets[:]))
 
-        w1_grouped = keep.tile([P, PACK, P, PACK], BF16, align_bytes=64)
-        deal_weight(nc.scalar.copy, w1_grouped, w1_raw[0], 0, 0, 64)
-        deal_weight(nc.vector.tensor_copy, w1_grouped, w1_raw[1], 1, 0, 32)
-        deal_weight(nc.scalar.copy, w1_grouped, w1_raw[1], 1, 32, 64)
-        w1_codes = keep.tile([P, WIDTH], U32, align_bytes=64)
-        w1_scale = keep.tile([P, WIDTH], U8, align_bytes=64)
+        w1_grouped = keep.tile([P, PACK, P, PACK], BF16, align_bytes=ALIGN)
+        deal_weight(nc.scalar.copy, w1_grouped, w1_raw[0], 0, 0, HALF_SLOT)
+        deal_weight(nc.vector.tensor_copy, w1_grouped, w1_raw[1], HALF_SLOT, 0, VECTOR_SHARE)
+        deal_weight(nc.scalar.copy, w1_grouped, w1_raw[1], HALF_SLOT, VECTOR_SHARE, HALF_SLOT)
+        w1_codes = keep.tile([P, WIDTH], U32, align_bytes=ALIGN)
+        w1_scale = keep.tile([P, WIDTH], U8, align_bytes=ALIGN)
         quantise(w1_grouped[:].rearrange("p t m j -> p (t m j)"), w1_codes[:], w1_scale[:])
 
-        w2_grouped = keep.tile([P, PACK, P, PACK], BF16, tag="w2_grouped", align_bytes=64)
+        w2_grouped = keep.tile([P, PACK, P, PACK], BF16, align_bytes=ALIGN)
 
         h_banks, g_grouped, h_rows, y_banks, results = [], [], [], [], []
 
@@ -97,30 +101,32 @@ def tile_picked_zres_gelu_po_kernel(tc, x_words, x_scales, w1, w2, turn, offs, o
 
         for c in range(CHUNKS):
             cols = slice(c * CHUNK, (c + 1) * CHUNK)
-            x_codes = keep.tile([P, CHUNK], U32, name="x_codes%d" % c, align_bytes=64)
-            nc.vector.tensor_copy(out=x_codes[:], in_=stored_words[:].bitcast(U32).indirect(offsets[:, c * CHUNK // 16 : (c + 1) * CHUNK // 16]))
+            entries = offsets[:, c * CHUNK // LIST_ROWS : (c + 1) * CHUNK // LIST_ROWS]
+            x_codes = keep.tile([P, CHUNK], U32, name="x_codes%d" % c, align_bytes=ALIGN)
+            nc.vector.tensor_copy(out=x_codes[:], in_=stored_words[:].bitcast(U32).indirect(entries))
             bank = psum.tile([P, PACK, CHUNK], F32, name="h_bank%d" % c)
             product(bank, w1_codes, w1_scale, x_codes[:], x_scale[:, cols])
             h_banks.append(bank)
             if c == CHUNKS - 1:
                 copy_h(0)
-            grouped = keep.tile([P, CHUNK, PACK], BF16, name="g_grouped%d" % c, align_bytes=64)
-            nc.scalar.activation(out=grouped[:], in_=bank[:].rearrange("p t n -> p n t"), func=GELU)
-            g_grouped.append(grouped)
+            g_chunk = keep.tile([P, CHUNK, PACK], BF16, name="g_grouped%d" % c, align_bytes=ALIGN)
+            nc.scalar.activation(out=g_chunk[:], in_=bank[:].rearrange("p t n -> p n t"), func=GELU)
+            g_grouped.append(g_chunk)
         for c in range(1, CHUNKS):
             copy_h(c)
 
-        w2_codes = keep.tile([P, WIDTH], U32, align_bytes=64)
-        w2_scale = keep.tile([P, WIDTH], U8, align_bytes=64)
-        deal_weight(nc.vector.tensor_copy, w2_grouped, w2_raw[0], 0, 0, 64)
-        quantise_half(w2_grouped, w2_codes, w2_scale, 0)
-        deal_weight(nc.vector.tensor_copy, w2_grouped, w2_raw[1], 1, 0, 64)
-        g_codes = keep.tile([P, PICKED], U32, tag="w2_raw1", align_bytes=64)
-        g_scale = keep.tile([P, PICKED], U8, align_bytes=64)
+        w2_codes = keep.tile([P, WIDTH], U32, align_bytes=ALIGN)
+        w2_scale = keep.tile([P, WIDTH], U8, align_bytes=ALIGN)
+        for i, (first, last) in enumerate(W2_PIECES):
+            deal_weight(nc.vector.tensor_copy, w2_grouped, w2_raw[i], first // PACK, 0, (last - first) // PACK)
+            if last == HALF:
+                quantise_half(w2_grouped, w2_codes, w2_scale, 0)
+        g_codes = keep.tile([P, PICKED], U32, tag="w2_raw%d" % (len(W2_PIECES) - 1), align_bytes=ALIGN)
+        g_scale = keep.tile([P, PICKED], U8, align_bytes=ALIGN)
 
         out_rows = out_0.rearrange("(p t) n -> p t n", t=PACK)
         out_words = out_1[0].rearrange("p n t -> p (n t)").bitcast(I32)
-        out_scale = keep.tile([P, PICKED], U8, align_bytes=64)
+        out_scale = keep.tile([P, PICKED], U8, align_bytes=ALIGN)
 
         def second_product(c):
             cols = slice(c * CHUNK, (c + 1) * CHUNK)
@@ -146,15 +152,15 @@ def tile_picked_zres_gelu_po_kernel(tc, x_words, x_scales, w1, w2, turn, offs, o
         for c in range(1, CHUNKS):
             combine(c)
 
-        out_grouped = keep.tile([P, PICKED * PACK], BF16, align_bytes=64)
-        out_codes = keep.tile([P, PICKED], U32, align_bytes=64)
+        out_grouped = keep.tile([P, PICKED * PACK], BF16, align_bytes=ALIGN)
+        out_codes = keep.tile([P, PICKED], U32, align_bytes=ALIGN)
         for c in range(CHUNKS):
-            grouped = out_grouped[:, c * CHUNK * PACK : (c + 1) * CHUNK * PACK]
+            out_chunk = out_grouped[:, c * CHUNK * PACK : (c + 1) * CHUNK * PACK]
             if c == 0:
-                nc.gpsimd.tensor_scalar(out=grouped.rearrange("p (n t) -> p n t", t=PACK), in0=results[c][:].rearrange("p t n -> p n t"),
+                nc.gpsimd.tensor_scalar(out=out_chunk.rearrange("p (n t) -> p n t", t=PACK), in0=results[c][:].rearrange("p t n -> p n t"),
                                         scalar1=1.0, scalar2=-0.0, op0=MULT, op1=ADD)
             else:
-                nc.scalar.copy(out=grouped.rearrange("p (a i t) -> p a t i", i=4, t=PACK), in_=results[c][:].rearrange("p t (a i) -> p a t i", i=4))
+                nc.scalar.copy(out=out_chunk.rearrange("p (a i t) -> p a t i", i=4, t=PACK), in_=results[c][:].rearrange("p t (a i) -> p a t i", i=4))
         for first, last in ((0, 2), (2, 3), (3, 4)):
             cols = slice(first * CHUNK, last * CHUNK)
             quantise(out_grouped[:, first * CHUNK * PACK : last * CHUNK * PACK], out_codes[:, cols], out_scale[:, cols])
@@ -163,4 +169,5 @@ def tile_picked_zres_gelu_po_kernel(tc, x_words, x_scales, w1, w2, turn, offs, o
             nc.sync.dma_start(out=out_words[:, cols], in_=out_codes[:, cols].bitcast(I32))
         for q in range(QUADRANTS):
             queue = nc.sync if q % 2 == 0 else nc.scalar
-            queue.dma_start(out=out_2[0, 4 * q : 4 * q + 4, :].bitcast(I32), in_=out_scale[32 * q : 32 * q + 4, :].bitcast(I32))
+            queue.dma_start(out=out_2[0, SCALE_ROWS * q : SCALE_ROWS * (q + 1), :].bitcast(I32),
+                            in_=out_scale[QUADRANT * q : QUADRANT * q + SCALE_ROWS, :].bitcast(I32))

from contextlib import ExitStack

import concourse.mybir as mybir

F32 = mybir.dt.float32
BF16 = mybir.dt.bfloat16
I32 = mybir.dt.int32
U32 = mybir.dt.uint32
U16 = mybir.dt.uint16
U8 = mybir.dt.uint8
FP8X4 = mybir.dt.float8_e4m3fn_x4
GELU = mybir.ActivationFunctionType.Gelu_apprx_tanh
MULT = mybir.AluOpType.mult
ADD = mybir.AluOpType.add

P = 128
PACK = 4
WIDTH = 512
STORED = 1024
PICKED = 512
CHUNK = 128
CHUNKS = PICKED // CHUNK
LIST_ROWS = 16
QUADRANTS = 4
QUADRANT = P // QUADRANTS
SCALE_ROWS = 4
HALF = WIDTH // 2
HALF_SLOT = HALF // PACK
ALIGN = 64

VECTOR_SHARE = 40
W2_PIECES = ((0, 256), (256, 384), (384, 512))

FLOPS = 2 * 2 * WIDTH * WIDTH * PICKED


def tile_picked_zres_gelu_po_kernel(tc, x_words, x_scales, w1, w2, turn, offs, out_0, out_1, out_2):
    nc = tc.nc
    with ExitStack() as ctx:
        keep = ctx.enter_context(tc.tile_pool(name="keep", bufs=1))
        psum = ctx.enter_context(tc.psum_pool(name="psum", bufs=1))

        def load_weight_piece(w, first, last, name):
            raw = keep.tile([P, PACK, last - first], F32, name=name, tag=name, align_bytes=ALIGN)
            nc.sync.dma_start(out=raw[:], in_=w.rearrange("(p j) c -> p j c", j=PACK)[:, :, first:last])
            return raw

        def deal_weight(copy, grouped, raw, base, first, last):
            copy(out=grouped[:, :, base + first : base + last, :].rearrange("p (u e) m j -> p u m j e", e=2),
                 in_=raw[:].rearrange("p j (m u e) -> p u m j e", u=2, e=2)[:, :, first:last])

        def quantise(values, codes, scales):
            nc.vector.quantize_mx(out=codes.bitcast(FP8X4), scales=scales, in_=values)

        def quantise_half(grouped, codes, scales, half):
            for t in range(PACK):
                cols = slice(t * P + half * HALF_SLOT, t * P + (half + 1) * HALF_SLOT)
                quantise(grouped[:, t, half * HALF_SLOT : (half + 1) * HALF_SLOT].rearrange("p m j -> p (m j)"), codes[:, cols], scales[:, cols])

        def product(bank, w_codes, w_scales, codes, scales):
            for t in range(PACK):
                cols = slice(t * P, (t + 1) * P)
                nc.tensor.matmul_mx(out=bank[:, t, :], lhsT=w_codes[:, cols].bitcast(FP8X4), lhsT_scale=w_scales[:, cols],
                                    rhs=codes.bitcast(FP8X4), rhs_scale=scales, start=True, stop=True)

        stored_scales = keep.tile([P, STORED], U8, align_bytes=ALIGN)
        nc.vector.memset(stored_scales[:].bitcast(I32), 0)

        offsets = keep.tile([P, PICKED // LIST_ROWS], U16)
        nc.sync.dma_start(offsets[:], offs)
        w1_raw = [load_weight_piece(w1, 0, HALF, "w1_raw0")]
        for q in range(QUADRANTS):
            nc.sync.dma_start(out=stored_scales[QUADRANT * q : QUADRANT * q + SCALE_ROWS, :].bitcast(I32),
                              in_=x_scales[0, SCALE_ROWS * q : SCALE_ROWS * (q + 1), :].bitcast(I32))
        w1_raw.append(load_weight_piece(w1, HALF, WIDTH, "w1_raw1"))
        stored_words = keep.tile([P, STORED], I32, align_bytes=ALIGN)
        nc.sync.dma_start(out=stored_words[:], in_=x_words[0].rearrange("p n t -> p (n t)").bitcast(I32))
        w2_raw = [load_weight_piece(w2, first, last, "w2_raw%d" % i) for i, (first, last) in enumerate(W2_PIECES)]
        turn_cols = keep.tile([P, PACK], F32)
        nc.sync.dma_start(out=turn_cols[:], in_=turn.rearrange("(p t) o -> p (t o)", t=PACK))

        x_scale = keep.tile([P, PICKED], U8, align_bytes=ALIGN)
        nc.vector.tensor_copy(out=x_scale[:], in_=stored_scales[:].indirect(offsets[:]))

        w1_grouped = keep.tile([P, PACK, P, PACK], BF16, align_bytes=ALIGN)
        deal_weight(nc.scalar.copy, w1_grouped, w1_raw[0], 0, 0, HALF_SLOT)
        deal_weight(nc.vector.tensor_copy, w1_grouped, w1_raw[1], HALF_SLOT, 0, VECTOR_SHARE)
        deal_weight(nc.scalar.copy, w1_grouped, w1_raw[1], HALF_SLOT, VECTOR_SHARE, HALF_SLOT)
        w1_codes = keep.tile([P, WIDTH], U32, align_bytes=ALIGN)
        w1_scale = keep.tile([P, WIDTH], U8, align_bytes=ALIGN)
        quantise(w1_grouped[:].rearrange("p t m j -> p (t m j)"), w1_codes[:], w1_scale[:])

        w2_grouped = keep.tile([P, PACK, P, PACK], BF16, align_bytes=ALIGN)

        h_banks, g_grouped, h_rows, y_banks, results = [], [], [], [], []

        def copy_h(c):
            h = keep.tile([P, PACK, CHUNK], F32, name="h%d" % c)
            nc.scalar.copy(out=h[:], in_=h_banks[c][:])
            h_rows.append(h)

        for c in range(CHUNKS):
            cols = slice(c * CHUNK, (c + 1) * CHUNK)
            entries = offsets[:, c * CHUNK // LIST_ROWS : (c + 1) * CHUNK // LIST_ROWS]
            x_codes = keep.tile([P, CHUNK], U32, name="x_codes%d" % c, align_bytes=ALIGN)
            nc.vector.tensor_copy(out=x_codes[:], in_=stored_words[:].bitcast(U32).indirect(entries))
            bank = psum.tile([P, PACK, CHUNK], F32, name="h_bank%d" % c)
            product(bank, w1_codes, w1_scale, x_codes[:], x_scale[:, cols])
            h_banks.append(bank)
            if c == CHUNKS - 1:
                copy_h(0)
            g_chunk = keep.tile([P, CHUNK, PACK], BF16, name="g_grouped%d" % c, align_bytes=ALIGN)
            nc.scalar.activation(out=g_chunk[:], in_=bank[:].rearrange("p t n -> p n t"), func=GELU)
            g_grouped.append(g_chunk)
        for c in range(1, CHUNKS):
            copy_h(c)

        w2_codes = keep.tile([P, WIDTH], U32, align_bytes=ALIGN)
        w2_scale = keep.tile([P, WIDTH], U8, align_bytes=ALIGN)
        for i, (first, last) in enumerate(W2_PIECES):
            deal_weight(nc.vector.tensor_copy, w2_grouped, w2_raw[i], first // PACK, 0, (last - first) // PACK)
            if last == HALF:
                quantise_half(w2_grouped, w2_codes, w2_scale, 0)
        g_codes = keep.tile([P, PICKED], U32, tag="w2_raw%d" % (len(W2_PIECES) - 1), align_bytes=ALIGN)
        g_scale = keep.tile([P, PICKED], U8, align_bytes=ALIGN)

        out_rows = out_0.rearrange("(p t) n -> p t n", t=PACK)
        out_words = out_1[0].rearrange("p n t -> p (n t)").bitcast(I32)
        out_scale = keep.tile([P, PICKED], U8, align_bytes=ALIGN)

        def second_product(c):
            cols = slice(c * CHUNK, (c + 1) * CHUNK)
            quantise(g_grouped[c][:].rearrange("p n t -> p (n t)"), g_codes[:, cols], g_scale[:, cols])
            if c == 0:
                quantise_half(w2_grouped, w2_codes, w2_scale, 1)
            bank = psum.tile([P, PACK, CHUNK], F32, name="y_bank%d" % c)
            product(bank, w2_codes, w2_scale, g_codes[:, cols], g_scale[:, cols])
            y_banks.append(bank)

        def combine(c):
            result = keep.tile([P, PACK, CHUNK], F32, name="result%d" % c)
            for t in range(PACK):
                nc.vector.scalar_tensor_tensor(out=result[:, t, :], in0=y_banks[c][:, t, :], scalar=turn_cols[:, t : t + 1],
                                               in1=h_rows[c][:, t, :], op0=MULT, op1=ADD)
            nc.sync.dma_start(out=out_rows[:, :, c * CHUNK : (c + 1) * CHUNK], in_=result[:])
            results.append(result)

        for c in range(CHUNKS - 1):
            second_product(c)
        combine(0)
        second_product(CHUNKS - 1)
        for c in range(1, CHUNKS):
            combine(c)

        out_grouped = keep.tile([P, PICKED * PACK], BF16, align_bytes=ALIGN)
        out_codes = keep.tile([P, PICKED], U32, align_bytes=ALIGN)
        for c in range(CHUNKS):
            out_chunk = out_grouped[:, c * CHUNK * PACK : (c + 1) * CHUNK * PACK]
            if c == 0:
                nc.gpsimd.tensor_scalar(out=out_chunk.rearrange("p (n t) -> p n t", t=PACK), in0=results[c][:].rearrange("p t n -> p n t"),
                                        scalar1=1.0, scalar2=-0.0, op0=MULT, op1=ADD)
            else:
                nc.scalar.copy(out=out_chunk.rearrange("p (a i t) -> p a t i", i=4, t=PACK), in_=results[c][:].rearrange("p t (a i) -> p a t i", i=4))
        for first, last in ((0, 2), (2, 3), (3, 4)):
            cols = slice(first * CHUNK, last * CHUNK)
            quantise(out_grouped[:, first * CHUNK * PACK : last * CHUNK * PACK], out_codes[:, cols], out_scale[:, cols])
        for half in range(2):
            cols = slice(half * PICKED // 2, (half + 1) * PICKED // 2)
            nc.sync.dma_start(out=out_words[:, cols], in_=out_codes[:, cols].bitcast(I32))
        for q in range(QUADRANTS):
            queue = nc.sync if q % 2 == 0 else nc.scalar
            queue.dma_start(out=out_2[0, SCALE_ROWS * q : SCALE_ROWS * (q + 1), :].bitcast(I32),
                            in_=out_scale[QUADRANT * q : QUADRANT * q + SCALE_ROWS, :].bitcast(I32))
